import numpy as np
import ml_dtypes


def mxq(x, axis, fmt="e4m3"):
    dtype, down = {"e4m3": (ml_dtypes.float8_e4m3fn, 7), "e5m2": (ml_dtypes.float8_e5m2, 14)}[fmt]
    v = np.moveaxis(np.asarray(x, np.float32).astype(ml_dtypes.bfloat16).astype(np.float64), axis, -1)
    blocks = v.reshape(v.shape[:-1] + (-1, 32))
    amax = np.abs(blocks).max(-1, keepdims=True)
    byte = np.maximum(np.where(amax > 0, np.frexp(amax)[1] - 1 + 127, 0) - down, 1)
    scale = np.exp2(byte - 127.0)
    codes = (blocks / scale).astype(np.float32).astype(dtype).astype(np.float64)
    return np.moveaxis((codes * scale).reshape(v.shape), -1, axis)


WIDE = False


def mx_kscale(k):
    if not WIDE:
        return np.ones(k)
    levels = np.array([10, -10, 5, -5, 0])
    if k % 512:
        return np.exp2(np.random.permutation(np.resize(levels, k // 32))).repeat(32)
    a = np.empty((k // 512, 16))
    for p in range(k // 512):
        a[p, :8] = np.random.permutation(np.resize(levels, 8))
        for g in range(8):
            far = levels[np.abs(levels - a[p, g]) >= 10]
            a[p, g + 8] = far[np.random.randint(len(far))]
    return np.exp2(a.ravel()).repeat(32)


def f64(x):
    return np.asarray(x).astype(np.float64)


def striped(idx):
    return np.tile(idx.reshape(-1, 16).T, (8, 1)).astype(np.uint16)


def unstriped(offs):
    return offs[:16].T.reshape(-1).astype(np.int64)


def pack_weight(w):
    k, n = w.shape
    w = f64(np.asarray(w, np.float32).astype(ml_dtypes.bfloat16)).reshape(k // 32, 32, n)
    amax = np.abs(w).max(1)
    byte = np.clip(np.where(amax > 0, np.frexp(amax)[1] - 1 + 127 - 7, 1), 1, 254)
    scaled = (w * np.exp2(127.0 - byte)[:, None, :]).reshape(k, n).astype(np.float32)
    words = np.ascontiguousarray(scaled.reshape(k // 512, 128, 4, n).transpose(0, 1, 3, 2)).astype(ml_dtypes.float8_e4m3fn).view(np.uint8)
    return words, np.ascontiguousarray(byte.astype(np.uint8).reshape(k // 512, 16, n))


def unpack_weight(words, scales):
    g, p, n, _ = words.shape
    vals = np.ascontiguousarray(words).view(ml_dtypes.float8_e4m3fn).astype(np.float64) * np.repeat(np.exp2(scales.astype(np.float64) - 127.0), 8, axis=1)[..., None]
    return vals.transpose(0, 1, 3, 2).reshape(g * 512, n)


K, T, S, N, H, W = 512, 2048, 512, 512, 512, 2048


def setup_inputs():
    n = np.random.standard_normal
    s = mx_kscale(K)[:, None]
    u = mx_kscale(S)
    packed_xT = pack_weight(n((K, T)) * s)
    return {
        "x_words": packed_xT[0],
        "x_scales": packed_xT[1],
        "wa": (n((K, H)) / np.sqrt(K) / s).astype(np.float32),
        "wb": (n((K, H)) / np.sqrt(K) / s).astype(np.float32),
        "gt": (np.random.uniform(0.5, 1.5, (S, 1)) * u[:, None]).astype(np.float32),
        "w1": (n((S, N)) / np.sqrt(S) / u[:, None]).astype(np.float32),
        "offs": striped(np.random.permutation(T)[:S]),
        "two": striped(np.random.permutation(T)[:S]),
        "n1": striped(np.random.permutation(H)),
        "n2": striped(np.random.permutation(H)),
        "n3": striped(np.random.randint(0, H, W)),
    }


def reference(x_words, x_scales, wa, wb, gt, w1, offs, two, n1, n2, n3):
    xq = unpack_weight(x_words, x_scales)[:, unstriped(offs)]
    y = xq.T @ mxq(f64(wa), 0, "e4m3")
    x_two = unpack_weight(x_words, x_scales)[:, unstriped(two)]
    d = x_two.T @ mxq(f64(wb), 0, "e4m3")
    z = f64(gt) * (np.maximum(y, d[:, unstriped(n2)]) - (np.minimum(y[:, unstriped(n1)], d)))
    h = mxq(f64(w1), 0, "e4m3").T @ mxq(z, 0, "e4m3")
    mb = h[:, unstriped(n3)]
    mx = mb.reshape(N, H, 4).max(axis=2)
    mn = mb.reshape(N, H, 4).min(axis=2)
    return mx * np.tanh(h - mn)

@@ -1,0 +1,236 @@
+from contextlib import ExitStack
+
+import concourse.mybir as mybir
+
+F32 = mybir.dt.float32
+BF16 = mybir.dt.bfloat16
+I32 = mybir.dt.int32
+U32 = mybir.dt.uint32
+U16 = mybir.dt.uint16
+U8 = mybir.dt.uint8
+FP8X4 = mybir.dt.float8_e4m3fn_x4
+ALU = mybir.AluOpType
+ACT = mybir.ActivationFunctionType
+
+FLOPS = 3 * 2 * 512 * 512 * 512
+
+P = 128
+PACK = 4
+T = 2048
+S = 512
+H = 512
+LANES = 16
+H_SPARE = 520
+HALF = 256
+Z_CHUNKS = (128, 128, 128, 128)
+N1_ON_SCALAR = (4, 4, 4, 4,)
+MEMBERS = 4
+OUT_PIECES = ((256, 256), (256, 256), (256, 256), (256, 128, 128))
+
+
+def weave(dst, src):
+    return (
+        dst.rearrange("p (c i t) -> p c t i", i=4, t=PACK),
+        src.rearrange("p t (c i) -> p c t i", i=4),
+    )
+
+
+def tile_picked_twtmaxbgtan_none_p_kernel(
+    tc, x_words, x_scales, wa, wb, gt, w1, offs, two, n1, n2, n3, out
+):
+    nc = tc.nc
+    with ExitStack() as ctx:
+        keep = ctx.enter_context(tc.tile_pool(name="keep", bufs=1))
+        ring = ctx.enter_context(tc.tile_pool(name="ring", bufs=2))
+        psum = ctx.enter_context(tc.psum_pool(name="psum", bufs=1))
+
+        def load_list(name, src):
+            tile = keep.tile(list(src.shape), U16, name=name)
+            nc.sync.dma_start(tile[:], src)
+            return tile
+
+        def entries(tile, first, count):
+            return tile[:, first // LANES : (first + count) // LANES]
+
+        def load_weight(name, w, c0, width):
+            raw = keep.tile([P, PACK, width], F32, name=name)
+            nc.sync.dma_start(raw[:], w[:, c0 : c0 + width].rearrange("(p t) c -> p t c", t=PACK))
+            return raw
+
+        landed = keep.tile([P, T], U8, name="landed")
+        for q in range(4):
+            nc.sync.dma_start(
+                landed[32 * q : 32 * q + 4, :].bitcast(I32),
+                x_scales[0, 4 * q : 4 * q + 4, :].bitcast(I32),
+            )
+        offs_t = load_list("offs_t", offs)
+        two_t = load_list("two_t", two)
+        wa_raw = [load_weight("wa_raw0", wa, 0, HALF)]
+        x_tab = keep.tile([P, T], I32, name="x_tab")
+        nc.sync.dma_start(x_tab[:], x_words[0].rearrange("p c r -> p (c r)").bitcast(I32))
+        wa_raw.append(load_weight("wa_raw1", wa, HALF, HALF))
+        wb_raw = [load_weight("wb_raw%d" % u, wb, u * HALF, HALF) for u in range(2)]
+        n1_t = load_list("n1_t", n1)
+        n2_t = load_list("n2_t", n2)
+        gate = keep.tile([P, PACK], F32, name="gate")
+        nc.sync.dma_start(gate[:], gt.rearrange("(p t) o -> p (t o)", t=PACK))
+        w1_raw = load_weight("w1_raw", w1, 0, H)
+        n3_t = load_list("n3_t", n3)
+
+        x_bytes = keep.tile([P, T], U8, name="x_bytes")
+        nc.vector.memset(x_bytes[:].bitcast(I32), 0)
+        y_all = keep.tile([P, PACK, H], F32, name="y_all")
+        d_all = keep.tile([P, PACK, H], F32, name="d_all")
+        h_rows = [keep.tile([P, H + H_SPARE], F32, name="h_row%d" % m) for m in range(4)]
+        for m in range(4):
+            nc.gpsimd.memset(h_rows[m][:, H:], 0.0)
+        for q in range(4):
+            rows = slice(32 * q, 32 * q + 4)
+            nc.vector.tensor_copy(x_bytes[rows, :].bitcast(I32), landed[rows, :].bitcast(I32))
+
+        def pick(name, lst, codes_tag):
+            picked = keep.tile([P, S], U8, name=name + "_picked")
+            nc.vector.tensor_copy(picked[:], x_bytes[:].indirect(lst[:]))
+            scales = keep.tile([P, S], U8, name=name + "_xscales", align_bytes=64)
+            codes = keep.tile([P, S], U32, name=codes_tag, align_bytes=64)
+            nc.vector.tensor_copy(
+                codes[:].rearrange("p (t m) -> p m t", t=PACK),
+                x_tab[:].bitcast(U32).indirect(lst[:]),
+            )
+            nc.vector.tensor_copy(
+                scales[:].rearrange("p (t m) -> p t m", t=PACK),
+                picked[:].rearrange("p (m t) -> p t m", t=PACK),
+            )
+            return codes, scales
+
+        def quantise(woven, codes, scales):
+            nc.vector.quantize_mx(out=codes.bitcast(FP8X4), scales=scales, in_=woven)
+
+        def weight_part(name, raw, copy, codes, scales):
+            width = raw.shape[2]
+            woven = keep.tile([P, PACK * width], BF16, name=name, align_bytes=64)
+            dst, src = weave(woven[:], raw)
+            copy(dst, src)
+            quantise(woven[:], codes, scales)
+
+        def mx_tiles(name, width):
+            codes = keep.tile([P, width], U32, name=name + "_codes", align_bytes=64)
+            scales = keep.tile([P, width], U8, name=name + "_scales", align_bytes=64)
+            return codes, scales
+
+        def product(bank, lhs, first, rhs_codes, rhs_scales):
+            nc.tensor.matmul_mx(
+                out=bank,
+                lhsT=lhs[0][:, first : first + P].bitcast(FP8X4),
+                lhsT_scale=lhs[1][:, first : first + P],
+                rhs=rhs_codes.bitcast(FP8X4),
+                rhs_scale=rhs_scales,
+                start=True,
+                stop=True,
+            )
+
+        x_offs = pick("offs", offs_t, "offs_xcodes")
+        wa_codes, wa_scales = mx_tiles("wa", H)
+        for u in range(2):
+            cols = slice(u * HALF, (u + 1) * HALF)
+            weight_part("wa_woven%d" % u, wa_raw[u][:], nc.scalar.copy, wa_codes[:, cols], wa_scales[:, cols])
+        x_two = pick("two", two_t, "wa_woven1")
+        wb_codes, wb_scales = mx_tiles("wb", H)
+        for u, copy in enumerate((nc.scalar.copy, nc.vector.tensor_copy)):
+            cols = slice(u * HALF, (u + 1) * HALF)
+            weight_part("wb_woven%d" % u, wb_raw[u][:], copy, wb_codes[:, cols], wb_scales[:, cols])
+
+        for t, copy in enumerate((nc.scalar.copy, nc.scalar.copy, nc.scalar.copy, nc.scalar.copy)):
+            bank = psum.tile([P, H], F32, name="bank%d" % t)
+            product(bank[:], x_offs, t * P, wa_codes[:], wa_scales[:])
+            copy(y_all[:, t, :], bank[:])
+        for t, copy in enumerate((nc.vector.tensor_copy, nc.vector.tensor_copy, nc.vector.tensor_copy, nc.scalar.copy)):
+            bank = psum.tile([P, H], F32, name="bank%d" % (PACK + t))
+            product(bank[:], x_two, t * P, wb_codes[:], wb_scales[:])
+            copy(d_all[:, t, :], bank[:])
+
+        w1_mx = mx_tiles("w1", H)
+
+        def w1_part(m0, count):
+            cols = slice(m0 * P, (m0 + count) * P)
+            weight_part("w1_woven%d" % m0, w1_raw[:, :, cols], nc.vector.tensor_copy, w1_mx[0][:, cols], w1_mx[1][:, cols])
+
+        w1_part(0, 1)
+
+        z_parts = []
+        c0 = 0
+        for k, cw in enumerate(Z_CHUNKS):
+            cols = slice(c0, c0 + cw)
+            d_n2 = keep.tile([P, PACK, cw], F32, name="d_n2_%d" % k)
+            upper = keep.tile([P, PACK, cw], F32, name="upper")
+            y_n1 = keep.tile([P, PACK, cw], F32, name="y_n1_%d" % k)
+            lower = keep.tile([P, PACK, cw], F32, name="lower")
+            for t in range(PACK):
+                if t < N1_ON_SCALAR[k]:
+                    nc.scalar.activation(y_n1[:, t, :], y_all[:, t, :].indirect(entries(n1_t, c0, cw)), ACT.Copy)
+                else:
+                    nc.vector.tensor_copy(y_n1[:, t, :], y_all[:, t, :].indirect(entries(n1_t, c0, cw)))
+            nc.vector.tensor_tensor(lower[:], d_all[:, :, cols], y_n1[:], ALU.min)
+            for t in range(PACK):
+                nc.scalar.activation(d_n2[:, t, :], d_all[:, t, :].indirect(entries(n2_t, c0, cw)), ACT.Copy)
+            spread = upper
+            step = 2 if cols.stop == H else PACK
+            for t0 in range(0, PACK, step):
+                ts = slice(t0, t0 + step)
+                nc.vector.tensor_tensor(upper[:, ts, :], y_all[:, ts, cols], d_n2[:, ts, :], ALU.max)
+                nc.vector.tensor_tensor(spread[:, ts, :], upper[:, ts, :], lower[:, ts, :], ALU.subtract)
+            z_woven = keep.tile([P, PACK * cw], BF16, name="z_woven%d" % k, align_bytes=64)
+            dst, src = weave(z_woven[:], spread[:])
+            nc.vector.tensor_tensor(
+                dst, src, gate[:].unsqueeze(1).unsqueeze(3).to_broadcast([P, cw // 4, PACK, 4]), ALU.mult
+            )
+            z_codes, z_scales = mx_tiles("z%d" % k, cw)
+            quantise(z_woven[:], z_codes[:], z_scales[:])
+            z_parts.append((cols, z_codes, z_scales))
+            c0 = c0 + cw
+
+        h_banks = []
+        for m in range(4):
+            if m > 0:
+                w1_part(m, 1)
+            bank = psum.tile([P, H], F32, name="bank%d" % (PACK + m))
+            for cols, z_codes, z_scales in z_parts:
+                product(bank[:, cols], w1_mx, m * P, z_codes[:], z_scales[:])
+                if m == 0 and cols.stop == H - Z_CHUNKS[-1]:
+                    nc.scalar.copy(h_rows[0][:, : cols.stop], bank[:, : cols.stop])
+                if m == 0 and cols.stop == H:
+                    nc.scalar.copy(h_rows[0][:, cols], bank[:, cols])
+            if m > 0:
+                nc.vector.tensor_copy(h_rows[m][:, :H], bank[:])
+            h_banks.append(bank)
+
+        def finish(m, cols, hi, bent):
+            res = ring.tile([P, hi.shape[1]], F32, name="res", bufs=3)
+            nc.vector.tensor_tensor(res[:], hi[:], bent[:], ALU.mult)
+            nc.sync.dma_start(out[m * P : (m + 1) * P, cols], res[:])
+
+        waiting = None
+        for m in range(4):
+            c0 = 0
+            for cw in OUT_PIECES[m]:
+                cols = slice(c0, c0 + cw)
+                flat = ring.tile([P, cw * MEMBERS], F32, name="members")
+                members = flat[:].rearrange("p (c t) -> p c t", t=MEMBERS)
+                nc.scalar.activation(flat[:], h_rows[m][:].indirect(entries(n3_t, c0 * MEMBERS, cw * MEMBERS)), ACT.Copy)
+                hi2 = ring.tile([P, cw, 2], F32, name="hi2", bufs=1)
+                lo2 = ring.tile([P, cw, 2], F32, name="lo2", bufs=1)
+                nc.vector.tensor_tensor(lo2[:], members[:, :, 0:2], members[:, :, 2:4], ALU.min)
+                nc.vector.tensor_tensor(hi2[:], members[:, :, 0:2], members[:, :, 2:4], ALU.max)
+                if waiting is not None:
+                    finish(*waiting)
+                hi = ring.tile([P, cw], F32, name="hi")
+                lo = flat[:, :cw]
+                nc.vector.tensor_tensor(lo, lo2[:, :, 0], lo2[:, :, 1], ALU.min)
+                nc.vector.tensor_tensor(hi[:], hi2[:, :, 0], hi2[:, :, 1], ALU.max)
+                gap = ring.tile([P, cw], F32, name="gap")
+                nc.vector.tensor_tensor(gap[:], h_banks[m][:, cols], lo, ALU.subtract)
+                bent = ring.tile([P, cw], F32, name="bent")
+                nc.scalar.activation(bent[:], gap[:], ACT.Tanh)
+                waiting = (m, cols, hi, bent)
+                c0 = c0 + cw
+        finish(*waiting)

@@ -23,7 +23,7 @@ LANES = 16
 H_SPARE = 520
 HALF = 256
 Z_CHUNKS = (128, 128, 128, 128)
-N1_ON_SCALAR = (4, 4, 4, 4,)
+N1_ON_SCALAR = (0, 4, 4, 4,)
 MEMBERS = 4
 OUT_PIECES = ((256, 256), (256, 256), (256, 256), (256, 128, 128))
 
@@ -65,11 +65,11 @@ def tile_picked_twtmaxbgtan_none_p_kernel(
             )
         offs_t = load_list("offs_t", offs)
         two_t = load_list("two_t", two)
-        wa_raw = [load_weight("wa_raw0", wa, 0, HALF)]
+        wa_raw = [load_weight("wa_raw%d" % u, wa, u * HALF, HALF) for u in range(2)]
+        wb_raw = [load_weight("wb_raw0", wb, 0, HALF)]
         x_tab = keep.tile([P, T], I32, name="x_tab")
         nc.sync.dma_start(x_tab[:], x_words[0].rearrange("p c r -> p (c r)").bitcast(I32))
-        wa_raw.append(load_weight("wa_raw1", wa, HALF, HALF))
-        wb_raw = [load_weight("wb_raw%d" % u, wb, u * HALF, HALF) for u in range(2)]
+        wb_raw.append(load_weight("wb_raw1", wb, HALF, HALF))
         n1_t = load_list("n1_t", n1)
         n2_t = load_list("n2_t", n2)
         gate = keep.tile([P, PACK], F32, name="gate")
@@ -79,7 +79,6 @@ def tile_picked_twtmaxbgtan_none_p_kernel(
 
         x_bytes = keep.tile([P, T], U8, name="x_bytes")
         nc.vector.memset(x_bytes[:].bitcast(I32), 0)
-        y_all = keep.tile([P, PACK, H], F32, name="y_all")
         d_all = keep.tile([P, PACK, H], F32, name="d_all")
         h_rows = [keep.tile([P, H + H_SPARE], F32, name="h_row%d" % m) for m in range(4)]
         for m in range(4):
@@ -134,103 +133,138 @@ def tile_picked_twtmaxbgtan_none_p_kernel(
         for u in range(2):
             cols = slice(u * HALF, (u + 1) * HALF)
             weight_part("wa_woven%d" % u, wa_raw[u][:], nc.scalar.copy, wa_codes[:, cols], wa_scales[:, cols])
-        x_two = pick("two", two_t, "wa_woven1")
+        x_two = pick("two", two_t, "two_xcodes")
         wb_codes, wb_scales = mx_tiles("wb", H)
-        for u, copy in enumerate((nc.scalar.copy, nc.vector.tensor_copy)):
+        for u, copy in enumerate((nc.scalar.copy, nc.scalar.copy)):
             cols = slice(u * HALF, (u + 1) * HALF)
             weight_part("wb_woven%d" % u, wb_raw[u][:], copy, wb_codes[:, cols], wb_scales[:, cols])
 
-        for t, copy in enumerate((nc.scalar.copy, nc.scalar.copy, nc.scalar.copy, nc.scalar.copy)):
+        y_all = keep.tile([P, PACK, H], F32, name="wb_raw1")
+        for t, copy in enumerate((nc.scalar.copy, nc.vector.tensor_copy, nc.scalar.copy, nc.vector.tensor_copy)):
             bank = psum.tile([P, H], F32, name="bank%d" % t)
             product(bank[:], x_offs, t * P, wa_codes[:], wa_scales[:])
             copy(y_all[:, t, :], bank[:])
-        for t, copy in enumerate((nc.vector.tensor_copy, nc.vector.tensor_copy, nc.vector.tensor_copy, nc.scalar.copy)):
+        for t, copy in enumerate((nc.scalar.copy, nc.vector.tensor_copy, nc.scalar.copy, nc.vector.tensor_copy)):
             bank = psum.tile([P, H], F32, name="bank%d" % (PACK + t))
             product(bank[:], x_two, t * P, wb_codes[:], wb_scales[:])
             copy(d_all[:, t, :], bank[:])
 
-        w1_mx = mx_tiles("w1", H)
-
-        def w1_part(m0, count):
-            cols = slice(m0 * P, (m0 + count) * P)
-            weight_part("w1_woven%d" % m0, w1_raw[:, :, cols], nc.vector.tensor_copy, w1_mx[0][:, cols], w1_mx[1][:, cols])
-
-        w1_part(0, 1)
-
-        z_parts = []
-        c0 = 0
+        starts = [sum(Z_CHUNKS[:k]) for k in range(len(Z_CHUNKS))]
+        fetched = []
         for k, cw in enumerate(Z_CHUNKS):
-            cols = slice(c0, c0 + cw)
-            d_n2 = keep.tile([P, PACK, cw], F32, name="d_n2_%d" % k)
-            upper = keep.tile([P, PACK, cw], F32, name="upper")
             y_n1 = keep.tile([P, PACK, cw], F32, name="y_n1_%d" % k)
-            lower = keep.tile([P, PACK, cw], F32, name="lower")
+            d_n2 = keep.tile([P, PACK, cw], F32, name="d_n2_%d" % k)
             for t in range(PACK):
                 if t < N1_ON_SCALAR[k]:
-                    nc.scalar.activation(y_n1[:, t, :], y_all[:, t, :].indirect(entries(n1_t, c0, cw)), ACT.Copy)
+                    nc.scalar.activation(y_n1[:, t, :], y_all[:, t, :].indirect(entries(n1_t, starts[k], cw)), ACT.Copy)
                 else:
-                    nc.vector.tensor_copy(y_n1[:, t, :], y_all[:, t, :].indirect(entries(n1_t, c0, cw)))
-            nc.vector.tensor_tensor(lower[:], d_all[:, :, cols], y_n1[:], ALU.min)
+                    nc.vector.tensor_copy(y_n1[:, t, :], y_all[:, t, :].indirect(entries(n1_t, starts[k], cw)))
             for t in range(PACK):
-                nc.scalar.activation(d_n2[:, t, :], d_all[:, t, :].indirect(entries(n2_t, c0, cw)), ACT.Copy)
-            spread = upper
-            step = 2 if cols.stop == H else PACK
-            for t0 in range(0, PACK, step):
-                ts = slice(t0, t0 + step)
-                nc.vector.tensor_tensor(upper[:, ts, :], y_all[:, ts, cols], d_n2[:, ts, :], ALU.max)
-                nc.vector.tensor_tensor(spread[:, ts, :], upper[:, ts, :], lower[:, ts, :], ALU.subtract)
-            z_woven = keep.tile([P, PACK * cw], BF16, name="z_woven%d" % k, align_bytes=64)
-            dst, src = weave(z_woven[:], spread[:])
-            nc.vector.tensor_tensor(
-                dst, src, gate[:].unsqueeze(1).unsqueeze(3).to_broadcast([P, cw // 4, PACK, 4]), ALU.mult
-            )
-            z_codes, z_scales = mx_tiles("z%d" % k, cw)
-            quantise(z_woven[:], z_codes[:], z_scales[:])
-            z_parts.append((cols, z_codes, z_scales))
-            c0 = c0 + cw
+                nc.scalar.activation(d_n2[:, t, :], d_all[:, t, :].indirect(entries(n2_t, starts[k], cw)), ACT.Copy)
+            fetched.append((y_n1, d_n2))
 
-        h_banks = []
-        for m in range(4):
-            if m > 0:
-                w1_part(m, 1)
-            bank = psum.tile([P, H], F32, name="bank%d" % (PACK + m))
-            for cols, z_codes, z_scales in z_parts:
-                product(bank[:, cols], w1_mx, m * P, z_codes[:], z_scales[:])
-                if m == 0 and cols.stop == H - Z_CHUNKS[-1]:
-                    nc.scalar.copy(h_rows[0][:, : cols.stop], bank[:, : cols.stop])
-                if m == 0 and cols.stop == H:
-                    nc.scalar.copy(h_rows[0][:, cols], bank[:, cols])
-            if m > 0:
-                nc.vector.tensor_copy(h_rows[m][:, :H], bank[:])
-            h_banks.append(bank)
+        w1_woven = []
+        for u in range(2):
+            woven = keep.tile([P, PACK * HALF], BF16, name="w1_woven%d" % u, align_bytes=64)
+            nc.scalar.copy(*weave(woven[:], w1_raw[:, :, u * HALF : (u + 1) * HALF]))
+            w1_woven.append(woven)
+
+        def smaller(k):
+            cw = Z_CHUNKS[k]
+            lower = ring.tile([P, PACK, cw], F32, name="lower")
+            nc.vector.tensor_tensor(lower[:], d_all[:, :, starts[k] : starts[k] + cw], fetched[k][0][:], ALU.min)
+            return lower
+
+        z_parts = []
+
+        def quantise_z(k, z_woven):
+            z_codes, z_scales = mx_tiles("z%d" % k, Z_CHUNKS[k])
+            quantise(z_woven[:], z_codes[:], z_scales[:])
+            z_parts.append((slice(starts[k], starts[k] + Z_CHUNKS[k]), z_codes, z_scales))
+
+        w1_mx = []
+
+        def quantise_w1(u, tag):
+            codes = keep.tile([P, HALF], U32, name=tag, align_bytes=64)
+            scales = keep.tile([P, HALF], U8, name="w1_scales%d" % u, align_bytes=64)
+            quantise(w1_woven[u][:], codes[:], scales[:])
+            w1_mx.append((codes, scales))
+
+        lower = smaller(0)
+        z_woven = None
+        for k, cw in enumerate(Z_CHUNKS):
+            upper = ring.tile([P, PACK, cw], F32, name="upper")
+            nc.vector.tensor_tensor(upper[:], y_all[:, :, starts[k] : starts[k] + cw], fetched[k][1][:], ALU.max)
+            if k > 0:
+                quantise_z(k - 1, z_woven)
+            nc.vector.tensor_tensor(upper[:], upper[:], lower[:], ALU.subtract)
+            if k + 1 < len(Z_CHUNKS):
+                lower = smaller(k + 1)
+            else:
+                quantise_w1(0, "z_woven2")
+            z_woven = keep.tile([P, PACK * cw], BF16, name="z_woven%d" % k, align_bytes=64)
+            nc.vector.tensor_tensor(
+                z_woven[:].rearrange("p (c i t) -> p c t i", i=2, t=PACK),
+                upper[:].rearrange("p t (c i) -> p c t i", i=2),
+                gate[:].unsqueeze(1).unsqueeze(3).to_broadcast([P, cw // 2, PACK, 2]),
+                ALU.mult,
+            )
+        quantise_z(len(Z_CHUNKS) - 1, z_woven)
+        quantise_w1(1, "z_woven3")
+
+        def make_h(m, parts, bank_name, copy):
+            bank = psum.tile([P, H], F32, name=bank_name)
+            for cols, z_codes, z_scales in parts:
+                product(bank[:, cols], w1_mx[m // 2], (m % 2) * P, z_codes[:], z_scales[:])
+            span = slice(parts[0][0].start, parts[-1][0].stop)
+            copy(h_rows[m][:, span], bank[:, span])
+
+        make_h(0, z_parts[:-1], "bank0", nc.scalar.copy)
+        make_h(0, z_parts[-1:], "bank1", nc.scalar.copy)
+        for m in range(1, 4):
+            make_h(m, z_parts, "bank%d" % (m + 1), nc.vector.tensor_copy)
+
+        def halve(single, pair, op):
+            nc.vector.tensor_tensor(single.rearrange("p (c i) -> p c i", i=2), pair[:, :, 0, :], pair[:, :, 1, :], op)
+
+        def pairwise(name, flat, op):
+            members = flat.rearrange("p (c i t) -> p c i t", i=2, t=MEMBERS)
+            pair = ring.tile([P, members.shape[1], 2, 2], F32, name=name, bufs=1)
+            nc.vector.tensor_tensor(
+                pair[:].rearrange("p c e i -> p c i e"), members[:, :, :, 0:2], members[:, :, :, 2:4], op
+            )
+            return pair
+
+        def largest(hi2):
+            hi = ring.tile([P, 2 * hi2.shape[1]], F32, name="hi", bufs=1)
+            halve(hi[:], hi2, ALU.max)
+            return hi
 
         def finish(m, cols, hi, bent):
             res = ring.tile([P, hi.shape[1]], F32, name="res", bufs=3)
             nc.vector.tensor_tensor(res[:], hi[:], bent[:], ALU.mult)
             nc.sync.dma_start(out[m * P : (m + 1) * P, cols], res[:])
 
-        waiting = None
+        before = None
+        spent = ring.tile([P, OUT_PIECES[0][0]], F32, name="members", bufs=3)
         for m in range(4):
             c0 = 0
             for cw in OUT_PIECES[m]:
                 cols = slice(c0, c0 + cw)
-                flat = ring.tile([P, cw * MEMBERS], F32, name="members")
-                members = flat[:].rearrange("p (c t) -> p c t", t=MEMBERS)
+                flat = ring.tile([P, cw * MEMBERS], F32, name="members", bufs=3)
                 nc.scalar.activation(flat[:], h_rows[m][:].indirect(entries(n3_t, c0 * MEMBERS, cw * MEMBERS)), ACT.Copy)
-                hi2 = ring.tile([P, cw, 2], F32, name="hi2", bufs=1)
-                lo2 = ring.tile([P, cw, 2], F32, name="lo2", bufs=1)
-                nc.vector.tensor_tensor(lo2[:], members[:, :, 0:2], members[:, :, 2:4], ALU.min)
-                nc.vector.tensor_tensor(hi2[:], members[:, :, 0:2], members[:, :, 2:4], ALU.max)
-                if waiting is not None:
-                    finish(*waiting)
-                hi = ring.tile([P, cw], F32, name="hi")
-                lo = flat[:, :cw]
-                nc.vector.tensor_tensor(lo, lo2[:, :, 0], lo2[:, :, 1], ALU.min)
-                nc.vector.tensor_tensor(hi[:], hi2[:, :, 0], hi2[:, :, 1], ALU.max)
+                lo2 = pairwise("lo2", flat[:], ALU.min)
+                if before is not None:
+                    hi = largest(before[2])
+                lo = spent[:, :cw]
+                halve(lo, lo2, ALU.min)
+                if before is not None:
+                    finish(before[0], before[1], hi, before[3])
                 gap = ring.tile([P, cw], F32, name="gap")
-                nc.vector.tensor_tensor(gap[:], h_banks[m][:, cols], lo, ALU.subtract)
+                nc.vector.tensor_tensor(gap[:], h_rows[m][:, cols], lo, ALU.subtract)
                 bent = ring.tile([P, cw], F32, name="bent")
                 nc.scalar.activation(bent[:], gap[:], ACT.Tanh)
-                waiting = (m, cols, hi, bent)
+                before = (m, cols, pairwise("hi2", flat[:], ALU.max), bent)
+                spent = flat
                 c0 = c0 + cw
-        finish(*waiting)
+        finish(before[0], before[1], largest(before[2]), before[3])

@@ -20,12 +20,12 @@ T = 2048
 S = 512
 H = 512
 LANES = 16
-H_SPARE = 520
+H_SPARE = 1024
 HALF = 256
 Z_CHUNKS = (128, 128, 128, 128)
 N1_ON_SCALAR = (0, 4, 4, 4,)
 MEMBERS = 4
-OUT_PIECES = ((256, 256), (256, 256), (256, 256), (256, 128, 128))
+OUT_PIECES = ((192, 320), (256, 256), (256, 256), (224, 192, 96))
 
 
 def weave(dst, src):
@@ -66,23 +66,23 @@ def tile_picked_twtmaxbgtan_none_p_kernel(
         offs_t = load_list("offs_t", offs)
         two_t = load_list("two_t", two)
         wa_raw = [load_weight("wa_raw%d" % u, wa, u * HALF, HALF) for u in range(2)]
-        wb_raw = [load_weight("wb_raw0", wb, 0, HALF)]
         x_tab = keep.tile([P, T], I32, name="x_tab")
         nc.sync.dma_start(x_tab[:], x_words[0].rearrange("p c r -> p (c r)").bitcast(I32))
-        wb_raw.append(load_weight("wb_raw1", wb, HALF, HALF))
+        wb_raw = [load_weight("wb_raw%d" % u, wb, u * HALF, HALF) for u in range(2)]
         n1_t = load_list("n1_t", n1)
         n2_t = load_list("n2_t", n2)
-        gate = keep.tile([P, PACK], F32, name="gate")
-        nc.sync.dma_start(gate[:], gt.rearrange("(p t) o -> p (t o)", t=PACK))
-        w1_raw = load_weight("w1_raw", w1, 0, H)
+        gate = keep.tile([P, PACK, 8], F32, name="gate")
+        w1_raw = keep.tile([P, PACK, H], F32, name="w1_raw")
+        for t in range(PACK):
+            nc.sync.dma_start(gate[:, t, 0:1], gt.rearrange("(q t b) o -> t q b o", t=PACK, b=4)[t])
+        for t in range(PACK):
+            nc.sync.dma_start(w1_raw[:, t, :], w1.rearrange("(q t b) c -> t q b c", t=PACK, b=4)[t])
         n3_t = load_list("n3_t", n3)
 
         x_bytes = keep.tile([P, T], U8, name="x_bytes")
         nc.vector.memset(x_bytes[:].bitcast(I32), 0)
         d_all = keep.tile([P, PACK, H], F32, name="d_all")
         h_rows = [keep.tile([P, H + H_SPARE], F32, name="h_row%d" % m) for m in range(4)]
-        for m in range(4):
-            nc.gpsimd.memset(h_rows[m][:, H:], 0.0)
         for q in range(4):
             rows = slice(32 * q, 32 * q + 4)
             nc.vector.tensor_copy(x_bytes[rows, :].bitcast(I32), landed[rows, :].bitcast(I32))
@@ -93,12 +93,12 @@ def tile_picked_twtmaxbgtan_none_p_kernel(
             scales = keep.tile([P, S], U8, name=name + "_xscales", align_bytes=64)
             codes = keep.tile([P, S], U32, name=codes_tag, align_bytes=64)
             nc.vector.tensor_copy(
-                codes[:].rearrange("p (t m) -> p m t", t=PACK),
+                codes[:].rearrange("p (t q b) -> p q t b", t=PACK, b=4),
                 x_tab[:].bitcast(U32).indirect(lst[:]),
             )
             nc.vector.tensor_copy(
-                scales[:].rearrange("p (t m) -> p t m", t=PACK),
-                picked[:].rearrange("p (m t) -> p t m", t=PACK),
+                scales[:].bitcast(I32).rearrange("p (t q) -> p t q", t=PACK),
+                picked[:].bitcast(I32).rearrange("p (q t) -> p t q", t=PACK),
             )
             return codes, scales
 
@@ -135,25 +135,29 @@ def tile_picked_twtmaxbgtan_none_p_kernel(
             weight_part("wa_woven%d" % u, wa_raw[u][:], nc.scalar.copy, wa_codes[:, cols], wa_scales[:, cols])
         x_two = pick("two", two_t, "two_xcodes")
         wb_codes, wb_scales = mx_tiles("wb", H)
-        for u, copy in enumerate((nc.scalar.copy, nc.scalar.copy)):
+        for u, copy in enumerate((nc.scalar.copy, nc.vector.tensor_copy)):
             cols = slice(u * HALF, (u + 1) * HALF)
             weight_part("wb_woven%d" % u, wb_raw[u][:], copy, wb_codes[:, cols], wb_scales[:, cols])
 
-        y_all = keep.tile([P, PACK, H], F32, name="wb_raw1")
-        for t, copy in enumerate((nc.scalar.copy, nc.vector.tensor_copy, nc.scalar.copy, nc.vector.tensor_copy)):
+        y_all = keep.tile([P, PACK, H], F32, name="wb_raw0")
+        for t, copy in enumerate((nc.scalar.copy, nc.scalar.copy, nc.scalar.copy, nc.scalar.copy)):
             bank = psum.tile([P, H], F32, name="bank%d" % t)
             product(bank[:], x_offs, t * P, wa_codes[:], wa_scales[:])
             copy(y_all[:, t, :], bank[:])
-        for t, copy in enumerate((nc.scalar.copy, nc.vector.tensor_copy, nc.scalar.copy, nc.vector.tensor_copy)):
-            bank = psum.tile([P, H], F32, name="bank%d" % (PACK + t))
-            product(bank[:], x_two, t * P, wb_codes[:], wb_scales[:])
-            copy(d_all[:, t, :], bank[:])
+        d_copies = ((nc.vector.tensor_copy, nc.vector.tensor_copy), (nc.scalar.copy, nc.vector.tensor_copy))
+        for u in range(2):
+            cols = slice(u * HALF, (u + 1) * HALF)
+            for v in range(2):
+                bank = psum.tile([P, 2, HALF], F32, name="bank%d" % (PACK + 2 * u + v))
+                for e in range(2):
+                    product(bank[:, e, :], x_two, (2 * v + e) * P, wb_codes[:, cols], wb_scales[:, cols])
+                d_copies[u][v](d_all[:, 2 * v : 2 * v + 2, cols], bank[:])
 
         starts = [sum(Z_CHUNKS[:k]) for k in range(len(Z_CHUNKS))]
         fetched = []
         for k, cw in enumerate(Z_CHUNKS):
-            y_n1 = keep.tile([P, PACK, cw], F32, name="y_n1_%d" % k)
-            d_n2 = keep.tile([P, PACK, cw], F32, name="d_n2_%d" % k)
+            y_n1 = h_rows[k][:, H : H + PACK * cw].rearrange("p (t c) -> p t c", t=PACK)
+            d_n2 = h_rows[k][:, H + PACK * cw :].rearrange("p (t c) -> p t c", t=PACK)
             for t in range(PACK):
                 if t < N1_ON_SCALAR[k]:
                     nc.scalar.activation(y_n1[:, t, :], y_all[:, t, :].indirect(entries(n1_t, starts[k], cw)), ACT.Copy)
@@ -172,7 +176,7 @@ def tile_picked_twtmaxbgtan_none_p_kernel(
         def smaller(k):
             cw = Z_CHUNKS[k]
             lower = ring.tile([P, PACK, cw], F32, name="lower")
-            nc.vector.tensor_tensor(lower[:], d_all[:, :, starts[k] : starts[k] + cw], fetched[k][0][:], ALU.min)
+            nc.vector.tensor_tensor(lower[:], d_all[:, :, starts[k] : starts[k] + cw], fetched[k][0], ALU.min)
             return lower
 
         z_parts = []
@@ -194,7 +198,7 @@ def tile_picked_twtmaxbgtan_none_p_kernel(
         z_woven = None
         for k, cw in enumerate(Z_CHUNKS):
             upper = ring.tile([P, PACK, cw], F32, name="upper")
-            nc.vector.tensor_tensor(upper[:], y_all[:, :, starts[k] : starts[k] + cw], fetched[k][1][:], ALU.max)
+            nc.vector.tensor_tensor(upper[:], y_all[:, :, starts[k] : starts[k] + cw], fetched[k][1], ALU.max)
             if k > 0:
                 quantise_z(k - 1, z_woven)
             nc.vector.tensor_tensor(upper[:], upper[:], lower[:], ALU.subtract)
@@ -206,7 +210,7 @@ def tile_picked_twtmaxbgtan_none_p_kernel(
             nc.vector.tensor_tensor(
                 z_woven[:].rearrange("p (c i t) -> p c t i", i=2, t=PACK),
                 upper[:].rearrange("p t (c i) -> p c t i", i=2),
-                gate[:].unsqueeze(1).unsqueeze(3).to_broadcast([P, cw // 2, PACK, 2]),
+                gate[:, :, 0:1].unsqueeze(1).to_broadcast([P, cw // 2, PACK, 2]),
                 ALU.mult,
             )
         quantise_z(len(Z_CHUNKS) - 1, z_woven)

@@ -22,8 +22,9 @@ H = 512
 LANES = 16
 H_SPARE = 1024
 HALF = 256
-Z_CHUNKS = (128, 128, 128, 128)
-N1_ON_SCALAR = (0, 4, 4, 4,)
+Z_CHUNKS = (256, 256)
+N1_ON_VECTOR = ((1, 2, 3,), (),)
+GROUPS = ((slice(0, 2), slice(2, 4),), (slice(0, 2), slice(2, 4),),)
 MEMBERS = 4
 OUT_PIECES = ((192, 320), (256, 256), (256, 256), (224, 192, 96))
 
@@ -155,16 +156,22 @@ def tile_picked_twtmaxbgtan_none_p_kernel(
 
         starts = [sum(Z_CHUNKS[:k]) for k in range(len(Z_CHUNKS))]
         fetched = []
+        used = 0
         for k, cw in enumerate(Z_CHUNKS):
-            y_n1 = h_rows[k][:, H : H + PACK * cw].rearrange("p (t c) -> p t c", t=PACK)
-            d_n2 = h_rows[k][:, H + PACK * cw :].rearrange("p (t c) -> p t c", t=PACK)
-            for t in range(PACK):
-                if t < N1_ON_SCALAR[k]:
-                    nc.scalar.activation(y_n1[:, t, :], y_all[:, t, :].indirect(entries(n1_t, starts[k], cw)), ACT.Copy)
-                else:
-                    nc.vector.tensor_copy(y_n1[:, t, :], y_all[:, t, :].indirect(entries(n1_t, starts[k], cw)))
-            for t in range(PACK):
-                nc.scalar.activation(d_n2[:, t, :], d_all[:, t, :].indirect(entries(n2_t, starts[k], cw)), ACT.Copy)
+            planes = []
+            for u in range(2):
+                at = H + used % H_SPARE
+                planes.append(h_rows[used // H_SPARE][:, at : at + PACK * cw].rearrange("p (t c) -> p t c", t=PACK))
+                used = used + PACK * cw
+            y_n1, d_n2 = planes
+            for ts in GROUPS[k]:
+                for t in range(ts.start, ts.stop):
+                    if t in N1_ON_VECTOR[k]:
+                        nc.vector.tensor_copy(y_n1[:, t, :], y_all[:, t, :].indirect(entries(n1_t, starts[k], cw)))
+                    else:
+                        nc.scalar.activation(y_n1[:, t, :], y_all[:, t, :].indirect(entries(n1_t, starts[k], cw)), ACT.Copy)
+                for t in range(ts.start, ts.stop):
+                    nc.scalar.activation(d_n2[:, t, :], d_all[:, t, :].indirect(entries(n2_t, starts[k], cw)), ACT.Copy)
             fetched.append((y_n1, d_n2))
 
         w1_woven = []
@@ -173,19 +180,7 @@ def tile_picked_twtmaxbgtan_none_p_kernel(
             nc.scalar.copy(*weave(woven[:], w1_raw[:, :, u * HALF : (u + 1) * HALF]))
             w1_woven.append(woven)
 
-        def smaller(k):
-            cw = Z_CHUNKS[k]
-            lower = ring.tile([P, PACK, cw], F32, name="lower")
-            nc.vector.tensor_tensor(lower[:], d_all[:, :, starts[k] : starts[k] + cw], fetched[k][0], ALU.min)
-            return lower
-
         z_parts = []
-
-        def quantise_z(k, z_woven):
-            z_codes, z_scales = mx_tiles("z%d" % k, Z_CHUNKS[k])
-            quantise(z_woven[:], z_codes[:], z_scales[:])
-            z_parts.append((slice(starts[k], starts[k] + Z_CHUNKS[k]), z_codes, z_scales))
-
         w1_mx = []
 
         def quantise_w1(u, tag):
@@ -194,26 +189,47 @@ def tile_picked_twtmaxbgtan_none_p_kernel(
             quantise(w1_woven[u][:], codes[:], scales[:])
             w1_mx.append((codes, scales))
 
-        lower = smaller(0)
-        z_woven = None
-        for k, cw in enumerate(Z_CHUNKS):
-            upper = ring.tile([P, PACK, cw], F32, name="upper")
-            nc.vector.tensor_tensor(upper[:], y_all[:, :, starts[k] : starts[k] + cw], fetched[k][1], ALU.max)
-            if k > 0:
-                quantise_z(k - 1, z_woven)
-            nc.vector.tensor_tensor(upper[:], upper[:], lower[:], ALU.subtract)
-            if k + 1 < len(Z_CHUNKS):
-                lower = smaller(k + 1)
-            else:
-                quantise_w1(0, "z_woven2")
-            z_woven = keep.tile([P, PACK * cw], BF16, name="z_woven%d" % k, align_bytes=64)
+        def quantise_z(c0, z_woven):
+            z_codes, z_scales = mx_tiles("z%d" % c0, P)
+            quantise(z_woven[:], z_codes[:], z_scales[:])
+            z_parts.append((slice(c0, c0 + P), z_codes, z_scales))
+
+        def meet(name, rows, k, ts, other, op):
+            dst = ring.tile([P, ts.stop - ts.start, Z_CHUNKS[k]], F32, name=name, bufs=2)
+            nc.vector.tensor_tensor(dst[:], rows[:, ts, starts[k] : starts[k] + Z_CHUNKS[k]], other[:, ts, :], op)
+            return dst
+
+        def weigh(c0, src):
+            z_woven = keep.tile([P, PACK * P], BF16, name="z_woven%d" % (c0 // P), align_bytes=64)
             nc.vector.tensor_tensor(
                 z_woven[:].rearrange("p (c i t) -> p c t i", i=2, t=PACK),
-                upper[:].rearrange("p t (c i) -> p c t i", i=2),
-                gate[:, :, 0:1].unsqueeze(1).to_broadcast([P, cw // 2, PACK, 2]),
+                src.rearrange("p t (c i) -> p c t i", i=2),
+                gate[:, :, 0:1].unsqueeze(1).to_broadcast([P, P // 2, PACK, 2]),
                 ALU.mult,
             )
-        quantise_z(len(Z_CHUNKS) - 1, z_woven)
+            return z_woven
+
+        units = [(k, ts) for k in range(len(Z_CHUNKS)) for ts in GROUPS[k]]
+        pending = []
+        lower = meet("lower", d_all, units[0][0], units[0][1], fetched[0][0], ALU.min)
+        for n, (k, ts) in enumerate(units):
+            cw = Z_CHUNKS[k]
+            if ts.start == 0:
+                spread = ring.tile([P, PACK, cw], F32, name="spread", bufs=2)
+            upper = meet("upper", y_all, k, ts, fetched[k][1], ALU.max)
+            if pending:
+                quantise_z(*pending.pop(0))
+            nc.vector.tensor_tensor(spread[:, ts, :], upper[:], lower[:], ALU.subtract)
+            if n + 1 < len(units):
+                lower = meet("lower", d_all, units[n + 1][0], units[n + 1][1], fetched[units[n + 1][0]][0], ALU.min)
+            else:
+                quantise_w1(0, "z_woven1")
+            if ts.stop == PACK:
+                for c0 in range(0, cw, P):
+                    pending.append((starts[k] + c0, weigh(starts[k] + c0, spread[:, :, c0 : c0 + P])))
+                    if len(pending) > 1:
+                        quantise_z(*pending.pop(0))
+        quantise_z(*pending.pop(0))
         quantise_w1(1, "z_woven3")
 
         def make_h(m, parts, bank_name, copy):

@@ -1,6 +1,7 @@
 from contextlib import ExitStack
 
 import concourse.mybir as mybir
+from concourse.masks import make_identity
 
 F32 = mybir.dt.float32
 BF16 = mybir.dt.bfloat16
@@ -26,7 +27,7 @@ Z_CHUNKS = (256, 256)
 N1_ON_VECTOR = ((1, 2, 3,), (),)
 GROUPS = ((slice(0, 2), slice(2, 4),), (slice(0, 2), slice(2, 4),),)
 MEMBERS = 4
-OUT_PIECES = ((192, 320), (256, 256), (256, 256), (224, 192, 96))
+OUT_PIECES = ((256, 256), (256, 256), (256, 256), (224, 192, 96))
 
 
 def weave(dst, src):
@@ -64,9 +65,10 @@ def tile_picked_twtmaxbgtan_none_p_kernel(
                 landed[32 * q : 32 * q + 4, :].bitcast(I32),
                 x_scales[0, 4 * q : 4 * q + 4, :].bitcast(I32),
             )
+        wa_raw = [load_weight("wa_raw0", wa, 0, HALF)]
         offs_t = load_list("offs_t", offs)
         two_t = load_list("two_t", two)
-        wa_raw = [load_weight("wa_raw%d" % u, wa, u * HALF, HALF) for u in range(2)]
+        wa_raw.append(load_weight("wa_raw1", wa, HALF, HALF))
         x_tab = keep.tile([P, T], I32, name="x_tab")
         nc.sync.dma_start(x_tab[:], x_words[0].rearrange("p c r -> p (c r)").bitcast(I32))
         wb_raw = [load_weight("wb_raw%d" % u, wb, u * HALF, HALF) for u in range(2)]
@@ -257,34 +259,53 @@ def tile_picked_twtmaxbgtan_none_p_kernel(
 
         def largest(hi2):
             hi = ring.tile([P, 2 * hi2.shape[1]], F32, name="hi", bufs=1)
-            halve(hi[:], hi2, ALU.max)
+            halve(hi[:], hi2, ALU.min)
             return hi
+
+        ident = keep.tile([P, P], F32, name="ident")
+        make_identity(nc, ident[:])
+
+        def turn(dst, src, start, stop):
+            nc.tensor.matmul(dst, src, ident[:], start=start, stop=stop, is_transpose=True)
 
         def finish(m, cols, hi, bent):
             res = ring.tile([P, hi.shape[1]], F32, name="res", bufs=3)
-            nc.vector.tensor_tensor(res[:], hi[:], bent[:], ALU.mult)
+            nc.vector.tensor_tensor(res[:], hi[:], bent, ALU.mult)
             nc.sync.dma_start(out[m * P : (m + 1) * P, cols], res[:])
 
+        pieces = [(m, sum(OUT_PIECES[m][:u]), cw) for m in range(4) for u, cw in enumerate(OUT_PIECES[m])]
         before = None
         spent = ring.tile([P, OUT_PIECES[0][0]], F32, name="members", bufs=3)
-        for m in range(4):
-            c0 = 0
-            for cw in OUT_PIECES[m]:
-                cols = slice(c0, c0 + cw)
-                flat = ring.tile([P, cw * MEMBERS], F32, name="members", bufs=3)
-                nc.scalar.activation(flat[:], h_rows[m][:].indirect(entries(n3_t, c0 * MEMBERS, cw * MEMBERS)), ACT.Copy)
-                lo2 = pairwise("lo2", flat[:], ALU.min)
-                if before is not None:
-                    hi = largest(before[2])
-                lo = spent[:, :cw]
-                halve(lo, lo2, ALU.min)
+        for n, (m, c0, cw) in enumerate(pieces):
+            cols = slice(c0, c0 + cw)
+            flat = ring.tile([P, cw * MEMBERS], F32, name="members", bufs=3)
+            nc.scalar.activation(
+                flat[:], h_rows[m][:].indirect(entries(n3_t, c0 * MEMBERS, cw * MEMBERS)), ACT.Copy, scale=-1.0
+            )
+            lo2 = pairwise("lo2", flat[:], ALU.max)
+            if before is not None:
+                hi = largest(before[2])
+            lo = spent[:, :cw]
+            halve(lo, lo2, ALU.max)
+            bent = ring.tile([P, cw], F32, name="bent")
+            if n < len(pieces) - 3:
+                turned = psum.tile([P, cw], F32, name="bank%d" % (5 + n % 2))
+                for b in range(0, cw, P):
+                    turn(turned[:, b : b + P], h_rows[m][:, c0 + b : c0 + b + P], True, False)
+                    turn(turned[:, b : b + P], lo[:, b : b + P], False, True)
+                nc.scalar.activation(bent[:], turned[:], ACT.Tanh, scale=-1.0)
+                back = psum.tile([P, cw], F32, name="bank%d" % (7 * (n % 2)))
+                for b in range(0, cw, P):
+                    turn(back[:, b : b + P], bent[:, b : b + P], True, True)
+                hi2 = pairwise("hi2", flat[:], ALU.min)
                 if before is not None:
                     finish(before[0], before[1], hi, before[3])
+                before = (m, cols, hi2, back[:])
+            else:
+                finish(before[0], before[1], hi, before[3])
                 gap = ring.tile([P, cw], F32, name="gap")
-                nc.vector.tensor_tensor(gap[:], h_rows[m][:, cols], lo, ALU.subtract)
-                bent = ring.tile([P, cw], F32, name="bent")
-                nc.scalar.activation(bent[:], gap[:], ACT.Tanh)
-                before = (m, cols, pairwise("hi2", flat[:], ALU.max), bent)
-                spent = flat
-                c0 = c0 + cw
+                nc.vector.tensor_tensor(gap[:], h_rows[m][:, cols], lo, ALU.add)
+                nc.scalar.activation(bent[:], gap[:], ACT.Tanh, scale=-1.0)
+                before = (m, cols, pairwise("hi2", flat[:], ALU.min), bent[:])
+            spent = flat
         finish(before[0], before[1], largest(before[2]), before[3])

from contextlib import ExitStack

import concourse.mybir as mybir
from concourse.masks import make_identity

F32 = mybir.dt.float32
BF16 = mybir.dt.bfloat16
I32 = mybir.dt.int32
U32 = mybir.dt.uint32
U16 = mybir.dt.uint16
U8 = mybir.dt.uint8
FP8X4 = mybir.dt.float8_e4m3fn_x4
ALU = mybir.AluOpType
ACT = mybir.ActivationFunctionType

FLOPS = 3 * 2 * 512 * 512 * 512

P = 128
PACK = 4
T = 2048
S = 512
H = 512
LANES = 16
H_SPARE = 1024
HALF = 256
Z_CHUNKS = (256, 256)
N1_ON_VECTOR = ((1, 2, 3,), (),)
GROUPS = ((slice(0, 2), slice(2, 4),), (slice(0, 2), slice(2, 4),),)
MEMBERS = 4
OUT_PIECES = ((256, 256), (256, 256), (256, 256), (224, 192, 96))


def weave(dst, src):
    return (
        dst.rearrange("p (c i t) -> p c t i", i=4, t=PACK),
        src.rearrange("p t (c i) -> p c t i", i=4),
    )


def tile_picked_twtmaxbgtan_none_p_kernel(
    tc, x_words, x_scales, wa, wb, gt, w1, offs, two, n1, n2, n3, out
):
    nc = tc.nc
    with ExitStack() as ctx:
        keep = ctx.enter_context(tc.tile_pool(name="keep", bufs=1))
        ring = ctx.enter_context(tc.tile_pool(name="ring", bufs=2))
        psum = ctx.enter_context(tc.psum_pool(name="psum", bufs=1))

        def load_list(name, src):
            tile = keep.tile(list(src.shape), U16, name=name)
            nc.sync.dma_start(tile[:], src)
            return tile

        def entries(tile, first, count):
            return tile[:, first // LANES : (first + count) // LANES]

        def load_weight(name, w, c0, width):
            raw = keep.tile([P, PACK, width], F32, name=name)
            nc.sync.dma_start(raw[:], w[:, c0 : c0 + width].rearrange("(p t) c -> p t c", t=PACK))
            return raw

        landed = keep.tile([P, T], U8, name="landed")
        for q in range(4):
            nc.sync.dma_start(
                landed[32 * q : 32 * q + 4, :].bitcast(I32),
                x_scales[0, 4 * q : 4 * q + 4, :].bitcast(I32),
            )
        wa_raw = [load_weight("wa_raw0", wa, 0, HALF)]
        offs_t = load_list("offs_t", offs)
        two_t = load_list("two_t", two)
        wa_raw.append(load_weight("wa_raw1", wa, HALF, HALF))
        x_tab = keep.tile([P, T], I32, name="x_tab")
        nc.sync.dma_start(x_tab[:], x_words[0].rearrange("p c r -> p (c r)").bitcast(I32))
        wb_raw = [load_weight("wb_raw%d" % u, wb, u * HALF, HALF) for u in range(2)]
        n1_t = load_list("n1_t", n1)
        n2_t = load_list("n2_t", n2)
        gate = keep.tile([P, PACK, 8], F32, name="gate")
        w1_raw = keep.tile([P, PACK, H], F32, name="w1_raw")
        for t in range(PACK):
            nc.sync.dma_start(gate[:, t, 0:1], gt.rearrange("(q t b) o -> t q b o", t=PACK, b=4)[t])
        for t in range(PACK):
            nc.sync.dma_start(w1_raw[:, t, :], w1.rearrange("(q t b) c -> t q b c", t=PACK, b=4)[t])
        n3_t = load_list("n3_t", n3)

        x_bytes = keep.tile([P, T], U8, name="x_bytes")
        nc.vector.memset(x_bytes[:].bitcast(I32), 0)
        d_all = keep.tile([P, PACK, H], F32, name="d_all")
        h_rows = [keep.tile([P, H + H_SPARE], F32, name="h_row%d" % m) for m in range(4)]
        for q in range(4):
            rows = slice(32 * q, 32 * q + 4)
            nc.vector.tensor_copy(x_bytes[rows, :].bitcast(I32), landed[rows, :].bitcast(I32))

        def pick(name, lst, codes_tag):
            picked = keep.tile([P, S], U8, name=name + "_picked")
            nc.vector.tensor_copy(picked[:], x_bytes[:].indirect(lst[:]))
            scales = keep.tile([P, S], U8, name=name + "_xscales", align_bytes=64)
            codes = keep.tile([P, S], U32, name=codes_tag, align_bytes=64)
            nc.vector.tensor_copy(
                codes[:].rearrange("p (t q b) -> p q t b", t=PACK, b=4),
                x_tab[:].bitcast(U32).indirect(lst[:]),
            )
            nc.vector.tensor_copy(
                scales[:].bitcast(I32).rearrange("p (t q) -> p t q", t=PACK),
                picked[:].bitcast(I32).rearrange("p (q t) -> p t q", t=PACK),
            )
            return codes, scales

        def quantise(woven, codes, scales):
            nc.vector.quantize_mx(out=codes.bitcast(FP8X4), scales=scales, in_=woven)

        def weight_part(name, raw, copy, codes, scales):
            width = raw.shape[2]
            woven = keep.tile([P, PACK * width], BF16, name=name, align_bytes=64)
            dst, src = weave(woven[:], raw)
            copy(dst, src)
            quantise(woven[:], codes, scales)

        def mx_tiles(name, width):
            codes = keep.tile([P, width], U32, name=name + "_codes", align_bytes=64)
            scales = keep.tile([P, width], U8, name=name + "_scales", align_bytes=64)
            return codes, scales

        def product(bank, lhs, first, rhs_codes, rhs_scales):
            nc.tensor.matmul_mx(
                out=bank,
                lhsT=lhs[0][:, first : first + P].bitcast(FP8X4),
                lhsT_scale=lhs[1][:, first : first + P],
                rhs=rhs_codes.bitcast(FP8X4),
                rhs_scale=rhs_scales,
                start=True,
                stop=True,
            )

        x_offs = pick("offs", offs_t, "offs_xcodes")
        wa_codes, wa_scales = mx_tiles("wa", H)
        for u in range(2):
            cols = slice(u * HALF, (u + 1) * HALF)
            weight_part("wa_woven%d" % u, wa_raw[u][:], nc.scalar.copy, wa_codes[:, cols], wa_scales[:, cols])
        x_two = pick("two", two_t, "two_xcodes")
        wb_codes, wb_scales = mx_tiles("wb", H)
        for u, copy in enumerate((nc.scalar.copy, nc.vector.tensor_copy)):
            cols = slice(u * HALF, (u + 1) * HALF)
            weight_part("wb_woven%d" % u, wb_raw[u][:], copy, wb_codes[:, cols], wb_scales[:, cols])

        y_all = keep.tile([P, PACK, H], F32, name="wb_raw0")
        for t, copy in enumerate((nc.scalar.copy, nc.scalar.copy, nc.scalar.copy, nc.scalar.copy)):
            bank = psum.tile([P, H], F32, name="bank%d" % t)
            product(bank[:], x_offs, t * P, wa_codes[:], wa_scales[:])
            copy(y_all[:, t, :], bank[:])
        d_copies = ((nc.vector.tensor_copy, nc.vector.tensor_copy), (nc.scalar.copy, nc.vector.tensor_copy))
        for u in range(2):
            cols = slice(u * HALF, (u + 1) * HALF)
            for v in range(2):
                bank = psum.tile([P, 2, HALF], F32, name="bank%d" % (PACK + 2 * u + v))
                for e in range(2):
                    product(bank[:, e, :], x_two, (2 * v + e) * P, wb_codes[:, cols], wb_scales[:, cols])
                d_copies[u][v](d_all[:, 2 * v : 2 * v + 2, cols], bank[:])

        starts = [sum(Z_CHUNKS[:k]) for k in range(len(Z_CHUNKS))]
        fetched = []
        used = 0
        for k, cw in enumerate(Z_CHUNKS):
            planes = []
            for u in range(2):
                at = H + used % H_SPARE
                planes.append(h_rows[used // H_SPARE][:, at : at + PACK * cw].rearrange("p (t c) -> p t c", t=PACK))
                used = used + PACK * cw
            y_n1, d_n2 = planes
            for ts in GROUPS[k]:
                for t in range(ts.start, ts.stop):
                    if t in N1_ON_VECTOR[k]:
                        nc.vector.tensor_copy(y_n1[:, t, :], y_all[:, t, :].indirect(entries(n1_t, starts[k], cw)))
                    else:
                        nc.scalar.activation(y_n1[:, t, :], y_all[:, t, :].indirect(entries(n1_t, starts[k], cw)), ACT.Copy)
                for t in range(ts.start, ts.stop):
                    nc.scalar.activation(d_n2[:, t, :], d_all[:, t, :].indirect(entries(n2_t, starts[k], cw)), ACT.Copy)
            fetched.append((y_n1, d_n2))

        w1_woven = []
        for u in range(2):
            woven = keep.tile([P, PACK * HALF], BF16, name="w1_woven%d" % u, align_bytes=64)
            nc.scalar.copy(*weave(woven[:], w1_raw[:, :, u * HALF : (u + 1) * HALF]))
            w1_woven.append(woven)

        z_parts = []
        w1_mx = []

        def quantise_w1(u, tag):
            codes = keep.tile([P, HALF], U32, name=tag, align_bytes=64)
            scales = keep.tile([P, HALF], U8, name="w1_scales%d" % u, align_bytes=64)
            quantise(w1_woven[u][:], codes[:], scales[:])
            w1_mx.append((codes, scales))

        def quantise_z(c0, z_woven):
            z_codes, z_scales = mx_tiles("z%d" % c0, P)
            quantise(z_woven[:], z_codes[:], z_scales[:])
            z_parts.append((slice(c0, c0 + P), z_codes, z_scales))

        def meet(name, rows, k, ts, other, op):
            dst = ring.tile([P, ts.stop - ts.start, Z_CHUNKS[k]], F32, name=name, bufs=2)
            nc.vector.tensor_tensor(dst[:], rows[:, ts, starts[k] : starts[k] + Z_CHUNKS[k]], other[:, ts, :], op)
            return dst

        def weigh(c0, src):
            z_woven = keep.tile([P, PACK * P], BF16, name="z_woven%d" % (c0 // P), align_bytes=64)
            nc.vector.tensor_tensor(
                z_woven[:].rearrange("p (c i t) -> p c t i", i=2, t=PACK),
                src.rearrange("p t (c i) -> p c t i", i=2),
                gate[:, :, 0:1].unsqueeze(1).to_broadcast([P, P // 2, PACK, 2]),
                ALU.mult,
            )
            return z_woven

        units = [(k, ts) for k in range(len(Z_CHUNKS)) for ts in GROUPS[k]]
        pending = []
        lower = meet("lower", d_all, units[0][0], units[0][1], fetched[0][0], ALU.min)
        for n, (k, ts) in enumerate(units):
            cw = Z_CHUNKS[k]
            if ts.start == 0:
                spread = ring.tile([P, PACK, cw], F32, name="spread", bufs=2)
            upper = meet("upper", y_all, k, ts, fetched[k][1], ALU.max)
            if pending:
                quantise_z(*pending.pop(0))
            nc.vector.tensor_tensor(spread[:, ts, :], upper[:], lower[:], ALU.subtract)
            if n + 1 < len(units):
                lower = meet("lower", d_all, units[n + 1][0], units[n + 1][1], fetched[units[n + 1][0]][0], ALU.min)
            else:
                quantise_w1(0, "z_woven1")
            if ts.stop == PACK:
                for c0 in range(0, cw, P):
                    pending.append((starts[k] + c0, weigh(starts[k] + c0, spread[:, :, c0 : c0 + P])))
                    if len(pending) > 1:
                        quantise_z(*pending.pop(0))
        quantise_z(*pending.pop(0))
        quantise_w1(1, "z_woven3")

        def make_h(m, parts, bank_name, copy):
            bank = psum.tile([P, H], F32, name=bank_name)
            for cols, z_codes, z_scales in parts:
                product(bank[:, cols], w1_mx[m // 2], (m % 2) * P, z_codes[:], z_scales[:])
            span = slice(parts[0][0].start, parts[-1][0].stop)
            copy(h_rows[m][:, span], bank[:, span])

        make_h(0, z_parts[:-1], "bank0", nc.scalar.copy)
        make_h(0, z_parts[-1:], "bank1", nc.scalar.copy)
        for m in range(1, 4):
            make_h(m, z_parts, "bank%d" % (m + 1), nc.vector.tensor_copy)

        def halve(single, pair, op):
            nc.vector.tensor_tensor(single.rearrange("p (c i) -> p c i", i=2), pair[:, :, 0, :], pair[:, :, 1, :], op)

        def pairwise(name, flat, op):
            members = flat.rearrange("p (c i t) -> p c i t", i=2, t=MEMBERS)
            pair = ring.tile([P, members.shape[1], 2, 2], F32, name=name, bufs=1)
            nc.vector.tensor_tensor(
                pair[:].rearrange("p c e i -> p c i e"), members[:, :, :, 0:2], members[:, :, :, 2:4], op
            )
            return pair

        def largest(hi2):
            hi = ring.tile([P, 2 * hi2.shape[1]], F32, name="hi", bufs=1)
            halve(hi[:], hi2, ALU.min)
            return hi

        ident = keep.tile([P, P], F32, name="ident")
        make_identity(nc, ident[:])

        def turn(dst, src, start, stop):
            nc.tensor.matmul(dst, src, ident[:], start=start, stop=stop, is_transpose=True)

        def finish(m, cols, hi, bent):
            res = ring.tile([P, hi.shape[1]], F32, name="res", bufs=3)
            nc.vector.tensor_tensor(res[:], hi[:], bent, ALU.mult)
            nc.sync.dma_start(out[m * P : (m + 1) * P, cols], res[:])

        pieces = [(m, sum(OUT_PIECES[m][:u]), cw) for m in range(4) for u, cw in enumerate(OUT_PIECES[m])]
        before = None
        spent = ring.tile([P, OUT_PIECES[0][0]], F32, name="members", bufs=3)
        for n, (m, c0, cw) in enumerate(pieces):
            cols = slice(c0, c0 + cw)
            flat = ring.tile([P, cw * MEMBERS], F32, name="members", bufs=3)
            nc.scalar.activation(
                flat[:], h_rows[m][:].indirect(entries(n3_t, c0 * MEMBERS, cw * MEMBERS)), ACT.Copy, scale=-1.0
            )
            lo2 = pairwise("lo2", flat[:], ALU.max)
            if before is not None:
                hi = largest(before[2])
            lo = spent[:, :cw]
            halve(lo, lo2, ALU.max)
            bent = ring.tile([P, cw], F32, name="bent")
            if n < len(pieces) - 3:
                turned = psum.tile([P, cw], F32, name="bank%d" % (5 + n % 2))
                for b in range(0, cw, P):
                    turn(turned[:, b : b + P], h_rows[m][:, c0 + b : c0 + b + P], True, False)
                    turn(turned[:, b : b + P], lo[:, b : b + P], False, True)
                nc.scalar.activation(bent[:], turned[:], ACT.Tanh, scale=-1.0)
                back = psum.tile([P, cw], F32, name="bank%d" % (7 * (n % 2)))
                for b in range(0, cw, P):
                    turn(back[:, b : b + P], bent[:, b : b + P], True, True)
                hi2 = pairwise("hi2", flat[:], ALU.min)
                if before is not None:
                    finish(before[0], before[1], hi, before[3])
                before = (m, cols, hi2, back[:])
            else:
                finish(before[0], before[1], hi, before[3])
                gap = ring.tile([P, cw], F32, name="gap")
                nc.vector.tensor_tensor(gap[:], h_rows[m][:, cols], lo, ALU.add)
                nc.scalar.activation(bent[:], gap[:], ACT.Tanh, scale=-1.0)
                before = (m, cols, pairwise("hi2", flat[:], ALU.min), bent[:])
            spent = flat
        finish(before[0], before[1], largest(before[2]), before[3])
